import numpy as np, ml_dtypes
CORES = [2,10,50,58,66,74,122]
N = 7
C = 128
def setup_inputs(rng):
    x = rng.standard_normal((N, 128, C), dtype=np.float32) * (0.25 + np.abs(rng.standard_normal((N, 1, C), dtype=np.float32)))
    return {"x": x.astype(ml_dtypes.bfloat16)}
def setup_inputs_big(rng):
    d = setup_inputs(rng)
    for k in ("x",): d[k] = (d[k].astype(np.float32) * 1048576.0).astype(d[k].dtype)
    return d
def setup_inputs_small(rng):
    d = setup_inputs(rng)
    for k in ("x",): d[k] = (d[k].astype(np.float32) * (1 / 1048576.0)).astype(d[k].dtype)
    return d
def setup_inputs_apart(rng):
    d = setup_inputs(rng)
    f = (10.0 ** rng.permutation(np.linspace(-1.5, 1.5, N))).astype(np.float32).reshape(N, 1, 1)
    for k in ("x",): d[k] = (d[k].astype(np.float32) * f).astype(d[k].dtype)
    return d
def setup_inputs_mixed(rng):
    d = setup_inputs(rng)
    f = (10.0 ** rng.uniform(-3, 3, (N, 1, C))).astype(np.float32); shape = rng.integers(3, size=(N, 1, C))
    for k in ("x",):
        x = d[k].astype(np.float32)
        m = x.mean(axis=1, keepdims=True); level = m + np.sign(x - m) * np.abs(x - m).mean(axis=1, keepdims=True) * rng.uniform(0.9, 1.1, x.shape).astype(np.float32)
        other = x * np.where(rng.random(x.shape) < 0.016, 100.0, 1.0).astype(np.float32)
        d[k] = (np.where(shape == 1, level, np.where(shape == 2, other, x)) * f).astype(d[k].dtype)
    return d
def reference(x):
    X = x.astype(np.float64); U = X / np.sqrt((X ** 2).sum(axis=1, keepdims=True))
    y = np.full((N, C, N * C), np.nan)
    for r in range(N):
        for s in range(N):
            if s != r: y[r][:, C * s:C * s + C] = U[r].T @ U[s]
    return {"y": y.astype(ml_dtypes.bfloat16)}

@@ -1,0 +1,197 @@
+from concourse.bass import DstId, RemoteDMATransfer
+from concourse.mybir import AluOpType, ActivationFunctionType
+
+N = 7
+C = 128
+
+SCRATCH = {
+    "xall": ("sbuf", [128, N * C], "bfloat16"),
+    "sq": ("sbuf", [128, N * C], "bfloat16"),
+    "dg": ("sbuf", [128, N * C], "bfloat16"),
+    "rs": ("sbuf", [128, N * C], "float32"),
+    "yb": ("sbuf", [128, N * C], "bfloat16"),
+    "u": ("sbuf", [128, C], "bfloat16"),
+    "ones": ("sbuf", [128, C], "bfloat16"),
+    "ident": ("sbuf", [128, C], "bfloat16"),
+    "inv": ("sbuf", [128, 8], "float32"),
+}
+for _b in range(N):
+    SCRATCH["ps%d" % _b] = ("psum", [128, 512], "float32")
+
+SEMAPHORES = ["ld", "c1", "c2", "snt", "st"]
+for _b in range(N):
+    SEMAPHORES += ["arr%d" % _b, "a%d" % _b, "t%d" % _b, "v%d" % _b]
+
+_CACHE = {}
+
+
+def _links(topo, a, b):
+    ca, cb, d = topo.chip(a), topo.chip(b), topo.die(a)
+    if ca == cb:
+        return ()
+    if topo.mates(ca, cb):
+        return (("mate", ca, cb, d),)
+    if topo.same_plane(ca, cb):
+        return (("out", ca, d), ("in", cb, d))
+    m = [k for k in range(topo.CHIPS) if topo.mates(ca, k)][0]
+    return (("mate", ca, m, d), ("out", m, d), ("in", cb, d))
+
+
+def _timetable(topo, cores):
+    key = tuple(cores)
+    if key in _CACHE:
+        return _CACHE[key]
+    n = len(cores)
+    way = [[_links(topo, cores[i], cores[j]) if i != j else () for j in range(n)] for i in range(n)]
+    rounds = []
+
+    def fill(i, perm, busy):
+        if i == n:
+            bits = 0
+            for k in range(n):
+                bits |= 1 << (k * n + perm[k])
+            rounds.append((tuple(perm), bits))
+            return
+        for j in range(n):
+            if j == i or j in perm:
+                continue
+            if any(l in busy for l in way[i][j]):
+                continue
+            fill(i + 1, perm + [j], busy | set(way[i][j]))
+
+    fill(0, [], set())
+
+    def cover(chosen, used):
+        if len(chosen) == n - 1:
+            return chosen
+        j = min(k for k in range(1, n) if not (used >> k) & 1)
+        for perm, bits in rounds:
+            if perm[0] == j and not (bits & used):
+                got = cover(chosen + [perm], used | bits)
+                if got:
+                    return got
+        return None
+
+    table = cover([], 0)
+    if not table:
+        table = [tuple((i + p) % n for i in range(n)) for p in range(1, n)]
+    _CACHE[key] = table
+    return table
+
+
+def _mask(topo, cores, i):
+    m = -1
+    for j in range(len(cores)):
+        if j != i:
+            m &= topo.mask(cores[i], cores[j])
+    return m
+
+
+def rank_program(g, core, T, topo):
+    r = T.rank_of(core)
+    if r is None:
+        return
+    cores = list(T.cores)
+    table = _timetable(topo, cores)
+    dests = [table[p][r] for p in range(N - 1)]
+    blocks = [r] + [list(table[p]).index(r) for p in range(N - 1)]
+    engines = [bin(_mask(topo, cores, i)).count("1") for i in range(N)]
+    sem = T.sem
+    S, V, P, Q = g.scalar, g.vector, g.tensor, g.sync
+    A = [sem["a%d" % b] for b in range(N)]
+    TS = [sem["t%d" % b] for b in range(N)]
+    VS = [sem["v%d" % b] for b in range(N)]
+    PS = [T["ps%d" % b] for b in range(N)]
+
+    def col(t, s):
+        return t[:, s * C:(s + 1) * C]
+
+    def here(q, b):
+        if b == 0:
+            q.wait_ge(sem.ld, 16)
+        else:
+            q.wait_ge(sem["arr%d" % blocks[b]], engines[blocks[b]])
+
+    def first(b):
+        return 0 if b == 0 else 1
+
+    def square(b):
+        here(S, b)
+        S.activation(col(T.sq, blocks[b]), col(T.xall, blocks[b]), ActivationFunctionType.Square).then_inc(A[b], 1)
+
+    def gram(b):
+        here(P, b)
+        P.matmul(PS[b][:, 0:C], T.u[:], col(T.xall, blocks[b]), True, True).then_inc(TS[b], 1)
+
+    def sums(b):
+        P.wait_ge(A[b], 1)
+        P.matmul(PS[b][:, 2 * C:2 * C + 1], col(T.sq, blocks[b]), T.ones[:, 0:1], True, True).then_inc(TS[b], 1)
+
+    def diag(b):
+        V.wait_ge(TS[b], first(b) + 1)
+        V.reciprocal(T.inv[:, b:b + 1], PS[b][:, 2 * C:2 * C + 1]).then_inc(VS[b], 1)
+        V.wait_ge(VS[b], 1)
+        V.tensor_scalar(col(T.dg, blocks[b]), T.ident[:], T.inv[:, b:b + 1], None, AluOpType.mult).then_inc(VS[b], 1)
+
+    def spread(b):
+        P.wait_ge(VS[b], 2)
+        P.matmul(PS[b][:, C:2 * C], T.ones[:], col(T.dg, blocks[b]), True, True).then_inc(TS[b], 1)
+
+    def root(b):
+        S.wait_ge(TS[b], first(b) + 2)
+        S.activation(col(T.rs, blocks[b]), PS[b][:, C:2 * C], ActivationFunctionType.Sqrt).then_inc(A[b], 1)
+
+    def scale(b):
+        V.wait_ge(A[b], 2)
+        if b == 0:
+            V.tensor_tensor(T.u[:], col(T.xall, r), col(T.rs, r), AluOpType.mult).then_inc(VS[b], 1)
+        else:
+            V.tensor_tensor(col(T.yb, blocks[b]), PS[b][:, 0:C], col(T.rs, blocks[b]), AluOpType.mult).then_inc(VS[b], 1)
+
+    def store(q, b):
+        q.wait_ge(VS[b], 3)
+        q.dma_start(col(T.y, blocks[b]), col(T.yb, blocks[b])).then_inc(sem.st, 16)
+
+    Q.dma_start(col(T.xall, r), T.x[:]).then_inc(sem.ld, 16)
+    V.memset(T.ones[:], 1.0).then_inc(sem.c1, 1)
+    g.wait_ge(sem.c1, 1)
+    g.affine_select(T.ident[:], T.ones[:], [[-1, C]], AluOpType.is_equal, 0.0, 0, 1).then_inc(sem.c2, 1)
+
+    g.wait_ge(sem.ld, 16)
+    ids = []
+    for d in dests:
+        rid, pid, _se = topo.addr(cores[d])
+        ids.append(DstId(rid=rid, pnc=pid))
+    g.remote_dma_fused(
+        [RemoteDMATransfer(dst_ids=ids, dma_engine_mask=_mask(topo, cores, r), remote_sem=sem["arr%d" % r],
+                           srcs=[col(T.xall, r)], dsts=[col(T.xall, r) for _d in dests], alu_op=0)],
+        local_sem=sem.snt)
+
+    P.wait_ge(sem.c1, 1)
+    V.wait_ge(sem.c2, 1)
+    V.wait_ge(sem.ld, 16)
+    square(0)
+    sums(0)
+    diag(0)
+    spread(0)
+    root(0)
+    scale(0)
+    P.wait_ge(VS[0], 3)
+
+    for b in range(1, N):
+        square(b)
+        gram(b)
+        sums(b)
+        diag(b)
+        if b >= 2:
+            spread(b - 1)
+            root(b - 1)
+            scale(b - 1)
+            store(Q, b - 1)
+    spread(N - 1)
+    root(N - 1)
+    scale(N - 1)
+    store(S, N - 1)
+
+    g.wait_ge(sem.snt, engines[r])
+    g.wait_ge(sem.st, 16 * (N - 1))

@@ -3,6 +3,7 @@ from concourse.mybir import AluOpType, ActivationFunctionType
 
 N = 7
 C = 128
+RAW = 4
 
 SCRATCH = {
     "xall": ("sbuf", [128, N * C], "bfloat16"),
@@ -152,20 +153,25 @@ def rank_program(g, core, T, topo):
         q.wait_ge(VS[b], 3)
         q.dma_start(col(T.y, blocks[b]), col(T.yb, blocks[b])).then_inc(sem.st, 16)
 
+    def send(src, ids):
+        g.remote_dma_fused(
+            [RemoteDMATransfer(dst_ids=ids, dma_engine_mask=_mask(topo, cores, r), remote_sem=sem["arr%d" % r],
+                               srcs=[src], dsts=[col(T.xall, r) for _d in ids], alu_op=0)],
+            local_sem=sem.snt)
+
     Q.dma_start(col(T.xall, r), T.x[:]).then_inc(sem.ld, 16)
     V.memset(T.ones[:], 1.0).then_inc(sem.c1, 1)
     g.wait_ge(sem.c1, 1)
     g.affine_select(T.ident[:], T.ones[:], [[-1, C]], AluOpType.is_equal, 0.0, 0, 1).then_inc(sem.c2, 1)
 
-    g.wait_ge(sem.ld, 16)
     ids = []
     for d in dests:
         rid, pid, _se = topo.addr(cores[d])
         ids.append(DstId(rid=rid, pnc=pid))
-    g.remote_dma_fused(
-        [RemoteDMATransfer(dst_ids=ids, dma_engine_mask=_mask(topo, cores, r), remote_sem=sem["arr%d" % r],
-                           srcs=[col(T.xall, r)], dsts=[col(T.xall, r) for _d in dests], alu_op=0)],
-        local_sem=sem.snt)
+    g.wait_ge(sem.ld, 16)
+    send(col(T.xall, r), ids[:RAW])
+    g.wait_ge(VS[0], 3)
+    send(T.u[:], ids[RAW:])
 
     P.wait_ge(sem.c1, 1)
     V.wait_ge(sem.c2, 1)
@@ -178,7 +184,7 @@ def rank_program(g, core, T, topo):
     scale(0)
     P.wait_ge(VS[0], 3)
 
-    for b in range(1, N):
+    for b in range(1, RAW + 1):
         square(b)
         gram(b)
         sums(b)
@@ -188,10 +194,20 @@ def rank_program(g, core, T, topo):
             root(b - 1)
             scale(b - 1)
             store(Q, b - 1)
-    spread(N - 1)
-    root(N - 1)
-    scale(N - 1)
-    store(S, N - 1)
+    spread(RAW)
+    root(RAW)
+    scale(RAW)
+    store(Q, RAW)
 
-    g.wait_ge(sem.snt, engines[r])
+    for b in range(RAW + 1, N):
+        gram(b)
+        if (N - 1 - b) % 2:
+            S.wait_ge(TS[b], 1)
+            S.activation(col(T.yb, blocks[b]), PS[b][:, 0:C], ActivationFunctionType.Copy).then_inc(VS[b], 3)
+        else:
+            V.wait_ge(TS[b], 1)
+            V.tensor_copy(col(T.yb, blocks[b]), PS[b][:, 0:C]).then_inc(VS[b], 3)
+        store(S if b == N - 1 else Q, b)
+
+    g.wait_ge(sem.snt, 2 * engines[r])
     g.wait_ge(sem.st, 16 * (N - 1))

@@ -3,7 +3,7 @@ from concourse.mybir import AluOpType, ActivationFunctionType
 
 N = 7
 C = 128
-RAW = 4
+RAW = 3
 
 SCRATCH = {
     "xall": ("sbuf", [128, N * C], "bfloat16"),
@@ -103,6 +103,7 @@ def rank_program(g, core, T, topo):
     TS = [sem["t%d" % b] for b in range(N)]
     VS = [sem["v%d" % b] for b in range(N)]
     PS = [T["ps%d" % b] for b in range(N)]
+    raw = list(range(1, RAW + 1))
 
     def col(t, s):
         return t[:, s * C:(s + 1) * C]
@@ -120,17 +121,19 @@ def rank_program(g, core, T, topo):
         here(S, b)
         S.activation(col(T.sq, blocks[b]), col(T.xall, blocks[b]), ActivationFunctionType.Square).then_inc(A[b], 1)
 
-    def gram(b):
+    def gram(b, mine):
         here(P, b)
-        P.matmul(PS[b][:, 0:C], T.u[:], col(T.xall, blocks[b]), True, True).then_inc(TS[b], 1)
+        P.matmul(PS[b][:, 0:C], mine, col(T.xall, blocks[b]), True, True).then_inc(TS[b], 1)
 
     def sums(b):
         P.wait_ge(A[b], 1)
         P.matmul(PS[b][:, 2 * C:2 * C + 1], col(T.sq, blocks[b]), T.ones[:, 0:1], True, True).then_inc(TS[b], 1)
 
-    def diag(b):
+    def recip(b):
         V.wait_ge(TS[b], first(b) + 1)
         V.reciprocal(T.inv[:, b:b + 1], PS[b][:, 2 * C:2 * C + 1]).then_inc(VS[b], 1)
+
+    def diag(b):
         V.wait_ge(VS[b], 1)
         V.tensor_scalar(col(T.dg, blocks[b]), T.ident[:], T.inv[:, b:b + 1], None, AluOpType.mult).then_inc(VS[b], 1)
 
@@ -140,7 +143,11 @@ def rank_program(g, core, T, topo):
 
     def root(b):
         S.wait_ge(TS[b], first(b) + 2)
-        S.activation(col(T.rs, blocks[b]), PS[b][:, C:2 * C], ActivationFunctionType.Sqrt).then_inc(A[b], 1)
+        if b == 0:
+            S.activation(col(T.rs, r), PS[b][:, C:2 * C], ActivationFunctionType.Sqrt).then_inc(A[b], 1)
+        else:
+            S.activation(col(T.rs, blocks[b]), PS[b][:, C:2 * C], ActivationFunctionType.Sqrt,
+                         scale=T.inv[:, 0:1]).then_inc(A[b], 1)
 
     def scale(b):
         V.wait_ge(A[b], 2)
@@ -178,29 +185,29 @@ def rank_program(g, core, T, topo):
     V.wait_ge(sem.ld, 16)
     square(0)
     sums(0)
+    recip(0)
     diag(0)
     spread(0)
     root(0)
     scale(0)
-    P.wait_ge(VS[0], 3)
 
-    for b in range(1, RAW + 1):
+    for b in raw:
         square(b)
-        gram(b)
+        gram(b, col(T.xall, r))
         sums(b)
-        diag(b)
-        if b >= 2:
-            spread(b - 1)
-            root(b - 1)
-            scale(b - 1)
-            store(Q, b - 1)
-    spread(RAW)
-    root(RAW)
-    scale(RAW)
-    store(Q, RAW)
+        recip(b)
+        if b > 1:
+            diag(b - 1)
+    diag(RAW)
+    for b in raw:
+        spread(b)
+        root(b)
+        scale(b)
+        store(Q, b)
 
+    P.wait_ge(VS[0], 3)
     for b in range(RAW + 1, N):
-        gram(b)
+        gram(b, T.u[:])
         if (N - 1 - b) % 2:
             S.wait_ge(TS[b], 1)
             S.activation(col(T.yb, blocks[b]), PS[b][:, 0:C], ActivationFunctionType.Copy).then_inc(VS[b], 3)

@@ -3,10 +3,12 @@ from concourse.mybir import AluOpType, ActivationFunctionType
 
 N = 7
 C = 128
+W = 136
 RAW = 3
+MID = 1
 
 SCRATCH = {
-    "xall": ("sbuf", [128, N * C], "bfloat16"),
+    "xall": ("sbuf", [128, N * W], "bfloat16"),
     "sq": ("sbuf", [128, N * C], "bfloat16"),
     "dg": ("sbuf", [128, N * C], "bfloat16"),
     "rs": ("sbuf", [128, N * C], "float32"),
@@ -15,11 +17,12 @@ SCRATCH = {
     "ones": ("sbuf", [128, C], "bfloat16"),
     "ident": ("sbuf", [128, C], "bfloat16"),
     "inv": ("sbuf", [128, 8], "float32"),
+    "ln": ("sbuf", [128, 8], "float32"),
 }
-for _b in range(N):
+for _b in range(N + 1):
     SCRATCH["ps%d" % _b] = ("psum", [128, 512], "float32")
 
-SEMAPHORES = ["ld", "c1", "c2", "snt", "st"]
+SEMAPHORES = ["ld", "c1", "c2", "snt", "st", "tq", "vq", "tz", "vz"]
 for _b in range(N):
     SEMAPHORES += ["arr%d" % _b, "a%d" % _b, "t%d" % _b, "v%d" % _b]
 
@@ -102,11 +105,19 @@ def rank_program(g, core, T, topo):
     A = [sem["a%d" % b] for b in range(N)]
     TS = [sem["t%d" % b] for b in range(N)]
     VS = [sem["v%d" % b] for b in range(N)]
-    PS = [T["ps%d" % b] for b in range(N)]
+    PS = [T["ps%d" % b] for b in range(N + 1)]
     raw = list(range(1, RAW + 1))
+    mid = list(range(RAW + 1, RAW + MID + 1))
+    Act = ActivationFunctionType
 
     def col(t, s):
         return t[:, s * C:(s + 1) * C]
+
+    def xs(s, more=0):
+        return T.xall[:, s * W:s * W + C + more]
+
+    def extra(s):
+        return T.xall[:, s * W + C:s * W + C + 1]
 
     def here(q, b):
         if b == 0:
@@ -114,59 +125,35 @@ def rank_program(g, core, T, topo):
         else:
             q.wait_ge(sem["arr%d" % blocks[b]], engines[blocks[b]])
 
-    def first(b):
-        return 0 if b == 0 else 1
-
     def square(b):
         here(S, b)
-        S.activation(col(T.sq, blocks[b]), col(T.xall, blocks[b]), ActivationFunctionType.Square).then_inc(A[b], 1)
+        S.activation(col(T.sq, blocks[b]), xs(blocks[b]), Act.Square).then_inc(A[b], 1)
 
-    def gram(b, mine):
+    def sums(b, out, done):
+        P.matmul(out, col(T.sq, blocks[b]), T.ones[:, 0:1], True, True).then_inc(done, 1)
+
+    def gram(b):
         here(P, b)
-        P.matmul(PS[b][:, 0:C], mine, col(T.xall, blocks[b]), True, True).then_inc(TS[b], 1)
+        P.matmul(PS[b][:, 0:C], T.u[:], xs(blocks[b]), True, True).then_inc(TS[b], 1)
 
-    def sums(b):
-        P.wait_ge(A[b], 1)
-        P.matmul(PS[b][:, 2 * C:2 * C + 1], col(T.sq, blocks[b]), T.ones[:, 0:1], True, True).then_inc(TS[b], 1)
+    def diag(b, value):
+        V.tensor_scalar(col(T.dg, blocks[b]), T.ident[:], value, None, AluOpType.mult).then_inc(VS[b], 1)
 
-    def recip(b):
-        V.wait_ge(TS[b], first(b) + 1)
-        V.reciprocal(T.inv[:, b:b + 1], PS[b][:, 2 * C:2 * C + 1]).then_inc(VS[b], 1)
-
-    def diag(b):
-        V.wait_ge(VS[b], 1)
-        V.tensor_scalar(col(T.dg, blocks[b]), T.ident[:], T.inv[:, b:b + 1], None, AluOpType.mult).then_inc(VS[b], 1)
-
-    def spread(b):
-        P.wait_ge(VS[b], 2)
+    def spread(b, ready):
+        P.wait_ge(VS[b], ready)
         P.matmul(PS[b][:, C:2 * C], T.ones[:], col(T.dg, blocks[b]), True, True).then_inc(TS[b], 1)
-
-    def root(b):
-        S.wait_ge(TS[b], first(b) + 2)
-        if b == 0:
-            S.activation(col(T.rs, r), PS[b][:, C:2 * C], ActivationFunctionType.Sqrt).then_inc(A[b], 1)
-        else:
-            S.activation(col(T.rs, blocks[b]), PS[b][:, C:2 * C], ActivationFunctionType.Sqrt,
-                         scale=T.inv[:, 0:1]).then_inc(A[b], 1)
-
-    def scale(b):
-        V.wait_ge(A[b], 2)
-        if b == 0:
-            V.tensor_tensor(T.u[:], col(T.xall, r), col(T.rs, r), AluOpType.mult).then_inc(VS[b], 1)
-        else:
-            V.tensor_tensor(col(T.yb, blocks[b]), PS[b][:, 0:C], col(T.rs, blocks[b]), AluOpType.mult).then_inc(VS[b], 1)
 
     def store(q, b):
         q.wait_ge(VS[b], 3)
         q.dma_start(col(T.y, blocks[b]), col(T.yb, blocks[b])).then_inc(sem.st, 16)
 
-    def send(src, ids):
+    def send(src, ids, more=0):
         g.remote_dma_fused(
             [RemoteDMATransfer(dst_ids=ids, dma_engine_mask=_mask(topo, cores, r), remote_sem=sem["arr%d" % r],
-                               srcs=[src], dsts=[col(T.xall, r) for _d in ids], alu_op=0)],
+                               srcs=[src], dsts=[xs(r, more) for _d in ids], alu_op=0)],
             local_sem=sem.snt)
 
-    Q.dma_start(col(T.xall, r), T.x[:]).then_inc(sem.ld, 16)
+    Q.dma_start(xs(r), T.x[:]).then_inc(sem.ld, 16)
     V.memset(T.ones[:], 1.0).then_inc(sem.c1, 1)
     g.wait_ge(sem.c1, 1)
     g.affine_select(T.ident[:], T.ones[:], [[-1, C]], AluOpType.is_equal, 0.0, 0, 1).then_inc(sem.c2, 1)
@@ -176,45 +163,66 @@ def rank_program(g, core, T, topo):
         rid, pid, _se = topo.addr(cores[d])
         ids.append(DstId(rid=rid, pnc=pid))
     g.wait_ge(sem.ld, 16)
-    send(col(T.xall, r), ids[:RAW])
+    send(xs(r), ids[:RAW])
+    g.wait_ge(sem.vz, 2)
+    send(xs(r, 1), ids[RAW:RAW + MID], 1)
     g.wait_ge(VS[0], 3)
-    send(T.u[:], ids[RAW:])
+    send(T.u[:], ids[RAW + MID:])
 
     P.wait_ge(sem.c1, 1)
     V.wait_ge(sem.c2, 1)
     V.wait_ge(sem.ld, 16)
     square(0)
-    sums(0)
-    recip(0)
-    diag(0)
-    spread(0)
-    root(0)
-    scale(0)
+    P.wait_ge(A[0], 1)
+    sums(0, PS[0][:, 2 * C:2 * C + 1], TS[0])
+    sums(0, PS[N][:, 0:1], sem.tz)
+    S.wait_ge(TS[0], 1)
+    S.activation(T.ln[:, 0:1], PS[0][:, 2 * C:2 * C + 1], Act.Sqrt).then_inc(A[0], 1)
+    V.wait_ge(sem.tz, 1)
+    V.reciprocal(T.inv[:, 7:8], PS[N][:, 0:1]).then_inc(sem.vz, 1)
+    V.wait_ge(sem.vz, 1)
+    V.tensor_copy(extra(r), T.inv[:, 7:8]).then_inc(sem.vz, 1)
+    V.wait_ge(A[0], 2)
+    V.reciprocal(T.inv[:, 0:1], T.ln[:, 0:1]).then_inc(VS[0], 1)
+    V.wait_ge(VS[0], 1)
+    diag(0, T.inv[:, 0:1])
+    spread(0, 2)
+    V.wait_ge(TS[0], 2)
+    V.tensor_tensor(T.u[:], xs(r), PS[0][:, C:2 * C], AluOpType.mult).then_inc(VS[0], 1)
 
+    P.wait_ge(sem.vz, 1)
     for b in raw:
         square(b)
-        gram(b, col(T.xall, r))
-        sums(b)
-        recip(b)
-        if b > 1:
-            diag(b - 1)
-    diag(RAW)
+        P.wait_ge(A[b], 1)
+        sums(b, PS[N][:, b:b + 1], sem.tq)
+    V.wait_ge(sem.tq, RAW)
+    V.reciprocal(T.inv[:, 1:RAW + 1], PS[N][:, 1:RAW + 1]).then_inc(sem.vq, 1)
+    V.wait_ge(sem.vq, 1)
+    P.wait_ge(VS[0], 3)
     for b in raw:
-        spread(b)
-        root(b)
-        scale(b)
+        diag(b, T.inv[:, b:b + 1])
+        gram(b)
+    for b in mid:
+        here(V, b)
+        diag(b, extra(blocks[b]))
+        gram(b)
+    for b in raw + mid:
+        spread(b, 1)
+        S.wait_ge(TS[b], 2)
+        S.activation(col(T.rs, blocks[b]), PS[b][:, C:2 * C], Act.Sqrt).then_inc(A[b], 2 if b in mid else 1)
+        V.wait_ge(A[b], 2)
+        V.tensor_tensor(col(T.yb, blocks[b]), PS[b][:, 0:C], col(T.rs, blocks[b]), AluOpType.mult).then_inc(VS[b], 2)
         store(Q, b)
 
-    P.wait_ge(VS[0], 3)
-    for b in range(RAW + 1, N):
-        gram(b, T.u[:])
+    for b in range(RAW + MID + 1, N):
+        gram(b)
         if (N - 1 - b) % 2:
             S.wait_ge(TS[b], 1)
-            S.activation(col(T.yb, blocks[b]), PS[b][:, 0:C], ActivationFunctionType.Copy).then_inc(VS[b], 3)
+            S.activation(col(T.yb, blocks[b]), PS[b][:, 0:C], Act.Copy).then_inc(VS[b], 3)
         else:
             V.wait_ge(TS[b], 1)
             V.tensor_copy(col(T.yb, blocks[b]), PS[b][:, 0:C]).then_inc(VS[b], 3)
         store(S if b == N - 1 else Q, b)
 
-    g.wait_ge(sem.snt, 2 * engines[r])
+    g.wait_ge(sem.snt, 3 * engines[r])
     g.wait_ge(sem.st, 16 * (N - 1))

from concourse.bass import DstId, RemoteDMATransfer
from concourse.mybir import AluOpType, ActivationFunctionType

N = 7
C = 128
W = 136
RAW = 3
MID = 1

SCRATCH = {
    "xall": ("sbuf", [128, N * W], "bfloat16"),
    "sq": ("sbuf", [128, N * C], "bfloat16"),
    "dg": ("sbuf", [128, N * C], "bfloat16"),
    "rs": ("sbuf", [128, N * C], "float32"),
    "yb": ("sbuf", [128, N * C], "bfloat16"),
    "u": ("sbuf", [128, C], "bfloat16"),
    "ones": ("sbuf", [128, C], "bfloat16"),
    "ident": ("sbuf", [128, C], "bfloat16"),
    "inv": ("sbuf", [128, 8], "float32"),
    "ln": ("sbuf", [128, 8], "float32"),
}
for _b in range(N + 1):
    SCRATCH["ps%d" % _b] = ("psum", [128, 512], "float32")

SEMAPHORES = ["ld", "c1", "c2", "snt", "st", "tq", "vq", "tz", "vz"]
for _b in range(N):
    SEMAPHORES += ["arr%d" % _b, "a%d" % _b, "t%d" % _b, "v%d" % _b]

_CACHE = {}


def _links(topo, a, b):
    ca, cb, d = topo.chip(a), topo.chip(b), topo.die(a)
    if ca == cb:
        return ()
    if topo.mates(ca, cb):
        return (("mate", ca, cb, d),)
    if topo.same_plane(ca, cb):
        return (("out", ca, d), ("in", cb, d))
    m = [k for k in range(topo.CHIPS) if topo.mates(ca, k)][0]
    return (("mate", ca, m, d), ("out", m, d), ("in", cb, d))


def _timetable(topo, cores):
    key = tuple(cores)
    if key in _CACHE:
        return _CACHE[key]
    n = len(cores)
    way = [[_links(topo, cores[i], cores[j]) if i != j else () for j in range(n)] for i in range(n)]
    rounds = []

    def fill(i, perm, busy):
        if i == n:
            bits = 0
            for k in range(n):
                bits |= 1 << (k * n + perm[k])
            rounds.append((tuple(perm), bits))
            return
        for j in range(n):
            if j == i or j in perm:
                continue
            if any(l in busy for l in way[i][j]):
                continue
            fill(i + 1, perm + [j], busy | set(way[i][j]))

    fill(0, [], set())

    def cover(chosen, used):
        if len(chosen) == n - 1:
            return chosen
        j = min(k for k in range(1, n) if not (used >> k) & 1)
        for perm, bits in rounds:
            if perm[0] == j and not (bits & used):
                got = cover(chosen + [perm], used | bits)
                if got:
                    return got
        return None

    table = cover([], 0)
    if not table:
        table = [tuple((i + p) % n for i in range(n)) for p in range(1, n)]
    _CACHE[key] = table
    return table


def _mask(topo, cores, i):
    m = -1
    for j in range(len(cores)):
        if j != i:
            m &= topo.mask(cores[i], cores[j])
    return m


def rank_program(g, core, T, topo):
    r = T.rank_of(core)
    if r is None:
        return
    cores = list(T.cores)
    table = _timetable(topo, cores)
    dests = [table[p][r] for p in range(N - 1)]
    blocks = [r] + [list(table[p]).index(r) for p in range(N - 1)]
    engines = [bin(_mask(topo, cores, i)).count("1") for i in range(N)]
    sem = T.sem
    S, V, P, Q = g.scalar, g.vector, g.tensor, g.sync
    A = [sem["a%d" % b] for b in range(N)]
    TS = [sem["t%d" % b] for b in range(N)]
    VS = [sem["v%d" % b] for b in range(N)]
    PS = [T["ps%d" % b] for b in range(N + 1)]
    raw = list(range(1, RAW + 1))
    mid = list(range(RAW + 1, RAW + MID + 1))
    Act = ActivationFunctionType

    def col(t, s):
        return t[:, s * C:(s + 1) * C]

    def xs(s, more=0):
        return T.xall[:, s * W:s * W + C + more]

    def extra(s):
        return T.xall[:, s * W + C:s * W + C + 1]

    def here(q, b):
        if b == 0:
            q.wait_ge(sem.ld, 16)
        else:
            q.wait_ge(sem["arr%d" % blocks[b]], engines[blocks[b]])

    def square(b):
        here(S, b)
        S.activation(col(T.sq, blocks[b]), xs(blocks[b]), Act.Square).then_inc(A[b], 1)

    def sums(b, out, done):
        P.matmul(out, col(T.sq, blocks[b]), T.ones[:, 0:1], True, True).then_inc(done, 1)

    def gram(b):
        here(P, b)
        P.matmul(PS[b][:, 0:C], T.u[:], xs(blocks[b]), True, True).then_inc(TS[b], 1)

    def diag(b, value):
        V.tensor_scalar(col(T.dg, blocks[b]), T.ident[:], value, None, AluOpType.mult).then_inc(VS[b], 1)

    def spread(b, ready):
        P.wait_ge(VS[b], ready)
        P.matmul(PS[b][:, C:2 * C], T.ones[:], col(T.dg, blocks[b]), True, True).then_inc(TS[b], 1)

    def store(q, b):
        q.wait_ge(VS[b], 3)
        q.dma_start(col(T.y, blocks[b]), col(T.yb, blocks[b])).then_inc(sem.st, 16)

    def send(src, ids, more=0):
        g.remote_dma_fused(
            [RemoteDMATransfer(dst_ids=ids, dma_engine_mask=_mask(topo, cores, r), remote_sem=sem["arr%d" % r],
                               srcs=[src], dsts=[xs(r, more) for _d in ids], alu_op=0)],
            local_sem=sem.snt)

    Q.dma_start(xs(r), T.x[:]).then_inc(sem.ld, 16)
    V.memset(T.ones[:], 1.0).then_inc(sem.c1, 1)
    g.wait_ge(sem.c1, 1)
    g.affine_select(T.ident[:], T.ones[:], [[-1, C]], AluOpType.is_equal, 0.0, 0, 1).then_inc(sem.c2, 1)

    ids = []
    for d in dests:
        rid, pid, _se = topo.addr(cores[d])
        ids.append(DstId(rid=rid, pnc=pid))
    g.wait_ge(sem.ld, 16)
    send(xs(r), ids[:RAW])
    g.wait_ge(sem.vz, 2)
    send(xs(r, 1), ids[RAW:RAW + MID], 1)
    g.wait_ge(VS[0], 3)
    send(T.u[:], ids[RAW + MID:])

    P.wait_ge(sem.c1, 1)
    V.wait_ge(sem.c2, 1)
    V.wait_ge(sem.ld, 16)
    square(0)
    P.wait_ge(A[0], 1)
    sums(0, PS[0][:, 2 * C:2 * C + 1], TS[0])
    sums(0, PS[N][:, 0:1], sem.tz)
    S.wait_ge(TS[0], 1)
    S.activation(T.ln[:, 0:1], PS[0][:, 2 * C:2 * C + 1], Act.Sqrt).then_inc(A[0], 1)
    V.wait_ge(sem.tz, 1)
    V.reciprocal(T.inv[:, 7:8], PS[N][:, 0:1]).then_inc(sem.vz, 1)
    V.wait_ge(sem.vz, 1)
    V.tensor_copy(extra(r), T.inv[:, 7:8]).then_inc(sem.vz, 1)
    V.wait_ge(A[0], 2)
    V.reciprocal(T.inv[:, 0:1], T.ln[:, 0:1]).then_inc(VS[0], 1)
    V.wait_ge(VS[0], 1)
    diag(0, T.inv[:, 0:1])
    spread(0, 2)
    V.wait_ge(TS[0], 2)
    V.tensor_tensor(T.u[:], xs(r), PS[0][:, C:2 * C], AluOpType.mult).then_inc(VS[0], 1)

    P.wait_ge(sem.vz, 1)
    for b in raw:
        square(b)
        P.wait_ge(A[b], 1)
        sums(b, PS[N][:, b:b + 1], sem.tq)
    V.wait_ge(sem.tq, RAW)
    V.reciprocal(T.inv[:, 1:RAW + 1], PS[N][:, 1:RAW + 1]).then_inc(sem.vq, 1)
    V.wait_ge(sem.vq, 1)
    P.wait_ge(VS[0], 3)
    for b in raw:
        diag(b, T.inv[:, b:b + 1])
        gram(b)
    for b in mid:
        here(V, b)
        diag(b, extra(blocks[b]))
        gram(b)
    for b in raw + mid:
        spread(b, 1)
        S.wait_ge(TS[b], 2)
        S.activation(col(T.rs, blocks[b]), PS[b][:, C:2 * C], Act.Sqrt).then_inc(A[b], 2 if b in mid else 1)
        V.wait_ge(A[b], 2)
        V.tensor_tensor(col(T.yb, blocks[b]), PS[b][:, 0:C], col(T.rs, blocks[b]), AluOpType.mult).then_inc(VS[b], 2)
        store(Q, b)

    for b in range(RAW + MID + 1, N):
        gram(b)
        if (N - 1 - b) % 2:
            S.wait_ge(TS[b], 1)
            S.activation(col(T.yb, blocks[b]), PS[b][:, 0:C], Act.Copy).then_inc(VS[b], 3)
        else:
            V.wait_ge(TS[b], 1)
            V.tensor_copy(col(T.yb, blocks[b]), PS[b][:, 0:C]).then_inc(VS[b], 3)
        store(S if b == N - 1 else Q, b)

    g.wait_ge(sem.snt, 3 * engines[r])
    g.wait_ge(sem.st, 16 * (N - 1))
